import numpy as np
CORES = [3,67,11,75,19,83,27,91,35,99,43,107,51,115,59,123]
N = 16
PERM = [[0,4],[1,5],[2,6],[3,7],[4,8],[5,9],[6,10],[7,11],[8,12],[9,13],[10,14],[11,15],[12,0],[13,1],[14,2],[15,3]]
def setup_inputs(rng):
    return {"x": rng.standard_normal((N, 128, 1024), dtype=np.float32)}
def reference(x):
    y = np.empty_like(x)
    for s, d in PERM:
        y[d] = x[s]
    return {"y": y}

@@ -1,0 +1,40 @@
+SCRATCH = {
+    "send": ("sbuf", [128, 1024], "float32"),
+    "land": ("sbuf", [128, 1024], "float32"),
+}
+SEMAPHORES = ["loaded", "read", "arrived", "stored"]
+
+
+def _engines(mask):
+    return bin(mask).count("1")
+
+
+def rank_program(g, core, T, topo):
+    rank = T.rank_of(core)
+    if rank is None:
+        return
+    perm = T.tables["PERM"]
+    dst = [d for s, d in perm if s == rank]
+    src = [s for s, d in perm if d == rank]
+
+    if dst and dst[0] == rank:
+        g.dma_start(T.y[:], T.x[:]).then_inc(T.sem.stored, 16)
+        g.wait_ge(T.sem.stored, 16)
+        return
+
+    sent = 0
+    if dst:
+        to = T.cores[dst[0]]
+        g.dma_start(T.send[:], T.x[:]).then_inc(T.sem.loaded, 16)
+        g.wait_ge(T.sem.loaded, 16)
+        rid, pid, _se = topo.addr(to)
+        mask = topo.mask(core, to)
+        g.remote_dma(T.land[:], T.send[:], T.sem.arrived, T.sem.read, pid, rid, mask)
+        sent = _engines(mask)
+    if src:
+        frm = T.cores[src[0]]
+        g.wait_ge(T.sem.arrived, _engines(topo.mask(frm, core)))
+        g.dma_start(T.y[:], T.land[:]).then_inc(T.sem.stored, 16)
+        g.wait_ge(T.sem.stored, 16)
+    if sent:
+        g.wait_ge(T.sem.read, sent)

@@ -1,40 +1,78 @@
+HALVES = 2
+ROWS = 64
 SCRATCH = {
-    "send": ("sbuf", [128, 1024], "float32"),
-    "land": ("sbuf", [128, 1024], "float32"),
+    "stage": ("dram", [HALVES, 128, 512], "float32"),
+    "relay": ("dram", [128, 512], "float32"),
+    "land": ("dram", [HALVES, 128, 512], "float32"),
 }
-SEMAPHORES = ["loaded", "read", "arrived", "stored"]
+SEMAPHORES = ["ld0", "ld1", "left", "handed", "arr0", "arr1", "stored"]
 
 
 def _engines(mask):
     return bin(mask).count("1")
 
 
+def _helper(rank_core, to, T, topo):
+    h = rank_core ^ 4
+    if topo.chip(rank_core) == topo.chip(to) or T.rank_of(h) is not None or not topo.may_write(h, to):
+        return None
+    return h
+
+
+def _write(g, T, topo, core, to, out, in_, remote_sem):
+    rid, pid, _se = topo.addr(to)
+    mask = topo.mask(core, to)
+    g.remote_dma(out, in_, remote_sem, T.sem.left, pid, rid, mask)
+    return _engines(mask)
+
+
 def rank_program(g, core, T, topo):
-    rank = T.rank_of(core)
-    if rank is None:
-        return
     perm = T.tables["PERM"]
-    dst = [d for s, d in perm if s == rank]
-    src = [s for s, d in perm if d == rank]
+    dst_of = {s: d for s, d in perm}
+    src_of = {d: s for s, d in perm}
+    rank = T.rank_of(core)
 
-    if dst and dst[0] == rank:
-        g.dma_start(T.y[:], T.x[:]).then_inc(T.sem.stored, 16)
-        g.wait_ge(T.sem.stored, 16)
+    if rank is None:
+        owner = T.rank_of(core ^ 4)
+        if owner is None or owner not in dst_of or dst_of[owner] == owner:
+            return
+        to = T.cores[dst_of[owner]]
+        if _helper(core ^ 4, to, T, topo) != core:
+            return
+        g.wait_ge(T.sem.handed, _engines(topo.mask(core ^ 4, core)))
+        n = _write(g, T, topo, core, to, T.land[1], T.relay[:], T.sem.arr1)
+        g.wait_ge(T.sem.left, n)
         return
 
-    sent = 0
-    if dst:
-        to = T.cores[dst[0]]
-        g.dma_start(T.send[:], T.x[:]).then_inc(T.sem.loaded, 16)
-        g.wait_ge(T.sem.loaded, 16)
-        rid, pid, _se = topo.addr(to)
-        mask = topo.mask(core, to)
-        g.remote_dma(T.land[:], T.send[:], T.sem.arrived, T.sem.read, pid, rid, mask)
-        sent = _engines(mask)
-    if src:
-        frm = T.cores[src[0]]
-        g.wait_ge(T.sem.arrived, _engines(topo.mask(frm, core)))
-        g.dma_start(T.y[:], T.land[:]).then_inc(T.sem.stored, 16)
-        g.wait_ge(T.sem.stored, 16)
-    if sent:
-        g.wait_ge(T.sem.read, sent)
+    if dst_of.get(rank) == rank:
+        g.sync.dma_start(T.y[0:ROWS, :], T.x[0:ROWS, :]).then_inc(T.sem.stored, 16)
+        g.scalar.dma_start(T.y[ROWS:2 * ROWS, :], T.x[ROWS:2 * ROWS, :]).then_inc(T.sem.stored, 16)
+        g.wait_ge(T.sem.stored, 32)
+        return
+
+    left = 0
+    if rank in dst_of:
+        to = T.cores[dst_of[rank]]
+        helper = _helper(core, to, T, topo)
+        g.sync.dma_start(T.stage[1], T.x[ROWS:2 * ROWS, :]).then_inc(T.sem.ld1, 16)
+        g.scalar.dma_start(T.stage[0], T.x[0:ROWS, :]).then_inc(T.sem.ld0, 16)
+        g.wait_ge(T.sem.ld1, 16)
+        if helper is not None:
+            left += _write(g, T, topo, core, helper, T.relay[:], T.stage[1], T.sem.handed)
+        else:
+            left += _write(g, T, topo, core, to, T.land[1], T.stage[1], T.sem.arr1)
+        g.wait_ge(T.sem.ld0, 16)
+        left += _write(g, T, topo, core, to, T.land[0], T.stage[0], T.sem.arr0)
+
+    if rank in src_of:
+        frm = T.cores[src_of[rank]]
+        frm1 = _helper(frm, core, T, topo)
+        if frm1 is None:
+            frm1 = frm
+        g.scalar.wait_ge(T.sem.arr0, _engines(topo.mask(frm, core)))
+        g.scalar.dma_start(T.y[0:ROWS, :], T.land[0]).then_inc(T.sem.stored, 16)
+        g.sync.wait_ge(T.sem.arr1, _engines(topo.mask(frm1, core)))
+        g.sync.dma_start(T.y[ROWS:2 * ROWS, :], T.land[1]).then_inc(T.sem.stored, 16)
+        g.wait_ge(T.sem.stored, 32)
+    if left:
+        g.wait_ge(T.sem.left, left)

HALVES = 2
ROWS = 64
SCRATCH = {
    "stage": ("dram", [HALVES, 128, 512], "float32"),
    "relay": ("dram", [128, 512], "float32"),
    "land": ("dram", [HALVES, 128, 512], "float32"),
}
SEMAPHORES = ["ld0", "ld1", "left", "handed", "arr0", "arr1", "stored"]


def _engines(mask):
    return bin(mask).count("1")


def _helper(rank_core, to, T, topo):
    h = rank_core ^ 4
    if topo.chip(rank_core) == topo.chip(to) or T.rank_of(h) is not None or not topo.may_write(h, to):
        return None
    return h


def _write(g, T, topo, core, to, out, in_, remote_sem):
    rid, pid, _se = topo.addr(to)
    mask = topo.mask(core, to)
    g.remote_dma(out, in_, remote_sem, T.sem.left, pid, rid, mask)
    return _engines(mask)


def rank_program(g, core, T, topo):
    perm = T.tables["PERM"]
    dst_of = {s: d for s, d in perm}
    src_of = {d: s for s, d in perm}
    rank = T.rank_of(core)

    if rank is None:
        owner = T.rank_of(core ^ 4)
        if owner is None or owner not in dst_of or dst_of[owner] == owner:
            return
        to = T.cores[dst_of[owner]]
        if _helper(core ^ 4, to, T, topo) != core:
            return
        g.wait_ge(T.sem.handed, _engines(topo.mask(core ^ 4, core)))
        n = _write(g, T, topo, core, to, T.land[1], T.relay[:], T.sem.arr1)
        g.wait_ge(T.sem.left, n)
        return

    if dst_of.get(rank) == rank:
        g.sync.dma_start(T.y[0:ROWS, :], T.x[0:ROWS, :]).then_inc(T.sem.stored, 16)
        g.scalar.dma_start(T.y[ROWS:2 * ROWS, :], T.x[ROWS:2 * ROWS, :]).then_inc(T.sem.stored, 16)
        g.wait_ge(T.sem.stored, 32)
        return

    left = 0
    if rank in dst_of:
        to = T.cores[dst_of[rank]]
        helper = _helper(core, to, T, topo)
        g.sync.dma_start(T.stage[1], T.x[ROWS:2 * ROWS, :]).then_inc(T.sem.ld1, 16)
        g.scalar.dma_start(T.stage[0], T.x[0:ROWS, :]).then_inc(T.sem.ld0, 16)
        g.wait_ge(T.sem.ld1, 16)
        if helper is not None:
            left += _write(g, T, topo, core, helper, T.relay[:], T.stage[1], T.sem.handed)
        else:
            left += _write(g, T, topo, core, to, T.land[1], T.stage[1], T.sem.arr1)
        g.wait_ge(T.sem.ld0, 16)
        left += _write(g, T, topo, core, to, T.land[0], T.stage[0], T.sem.arr0)

    if rank in src_of:
        frm = T.cores[src_of[rank]]
        frm1 = _helper(frm, core, T, topo)
        if frm1 is None:
            frm1 = frm
        g.scalar.wait_ge(T.sem.arr0, _engines(topo.mask(frm, core)))
        g.scalar.dma_start(T.y[0:ROWS, :], T.land[0]).then_inc(T.sem.stored, 16)
        g.sync.wait_ge(T.sem.arr1, _engines(topo.mask(frm1, core)))
        g.sync.dma_start(T.y[ROWS:2 * ROWS, :], T.land[1]).then_inc(T.sem.stored, 16)
        g.wait_ge(T.sem.stored, 32)
    if left:
        g.wait_ge(T.sem.left, left)
